import numpy as np
import ml_dtypes


def mxq(x, axis, fmt="e4m3"):
    dtype, down = {"e4m3": (ml_dtypes.float8_e4m3fn, 7), "e5m2": (ml_dtypes.float8_e5m2, 14)}[fmt]
    v = np.moveaxis(np.asarray(x, np.float32).astype(ml_dtypes.bfloat16).astype(np.float64), axis, -1)
    blocks = v.reshape(v.shape[:-1] + (-1, 32))
    amax = np.abs(blocks).max(-1, keepdims=True)
    byte = np.maximum(np.where(amax > 0, np.frexp(amax)[1] - 1 + 127, 0) - down, 1)
    scale = np.exp2(byte - 127.0)
    codes = (blocks / scale).astype(np.float32).astype(dtype).astype(np.float64)
    return np.moveaxis((codes * scale).reshape(v.shape), -1, axis)


WIDE = False


def mx_kscale(k):
    if not WIDE:
        return np.ones(k)
    levels = np.array([10, -10, 5, -5, 0])
    if k % 512:
        return np.exp2(np.random.permutation(np.resize(levels, k // 32))).repeat(32)
    a = np.empty((k // 512, 16))
    for p in range(k // 512):
        a[p, :8] = np.random.permutation(np.resize(levels, 8))
        for g in range(8):
            far = levels[np.abs(levels - a[p, g]) >= 10]
            a[p, g + 8] = far[np.random.randint(len(far))]
    return np.exp2(a.ravel()).repeat(32)


def f64(x):
    return np.asarray(x).astype(np.float64)


def striped(idx):
    return np.tile(idx.reshape(-1, 16).T, (8, 1)).astype(np.uint16)


def unstriped(offs):
    return offs[:16].T.reshape(-1).astype(np.int64)


def striped8(idx):
    return np.concatenate([x.reshape(-1, 16).T for x in idx]).astype(np.uint16)


def runs(offs, k):
    lists = np.stack([offs[16 * r : 16 * r + 16].T.reshape(-1) for r in range(8)]).astype(np.int64)
    return lists[np.arange(k) % 512 // 64]


def pack_weight(w):
    k, n = w.shape
    w = f64(np.asarray(w, np.float32).astype(ml_dtypes.bfloat16)).reshape(k // 32, 32, n)
    amax = np.abs(w).max(1)
    byte = np.clip(np.where(amax > 0, np.frexp(amax)[1] - 1 + 127 - 7, 1), 1, 254)
    scaled = (w * np.exp2(127.0 - byte)[:, None, :]).reshape(k, n).astype(np.float32)
    words = np.ascontiguousarray(scaled.reshape(k // 512, 128, 4, n).transpose(0, 1, 3, 2)).astype(ml_dtypes.float8_e4m3fn).view(np.uint8)
    return words, np.ascontiguousarray(byte.astype(np.uint8).reshape(k // 512, 16, n))


def unpack_weight(words, scales):
    g, p, n, _ = words.shape
    vals = np.ascontiguousarray(words).view(ml_dtypes.float8_e4m3fn).astype(np.float64) * np.repeat(np.exp2(scales.astype(np.float64) - 127.0), 8, axis=1)[..., None]
    return vals.transpose(0, 1, 3, 2).reshape(g * 512, n)


def sigmoid(v):
    return 1.0 / (1.0 + np.exp(-np.maximum(v, -700.0)))


K, T, S, N, H, W = 512, 2048, 512, 512, 512, 256


def setup_inputs():
    n = np.random.standard_normal
    s = mx_kscale(K)[:, None]
    u = mx_kscale(H)
    packed_xT = pack_weight(n((K, T)) * s)
    return {
        "x_words": packed_xT[0],
        "x_scales": packed_xT[1],
        "w1": (n((K, H)) / np.sqrt(K) / s).astype(np.float32),
        "w2": (n((K, H)) / np.sqrt(K) / s).astype(np.float32),
        "gn": (np.random.uniform(0.5, 1.5, (H, 1)) * u[:, None]).astype(np.float32),
        "w3": (n((H, N)) / np.sqrt(H) / u[:, None]).astype(np.float32),
        "offs": striped(np.random.permutation(T)[:S]),
        "hz": striped8(np.random.randint(0, T, (8, S))),
        "n1": striped(np.random.permutation(S)[:W]),
        "n2": striped(np.random.permutation(S)[:W]),
        "n3": striped8(np.stack([np.random.permutation(S) for _ in range(8)])),
        "n4": striped8(np.stack([np.random.permutation(S) for _ in range(8)])),
    }


def reference(x_words, x_scales, w1, w2, gn, w3, offs, hz, n1, n2, n3, n4):
    x_hz = unpack_weight(x_words, x_scales)[np.arange(K)[:, None], runs(hz, K)]
    d = mxq(f64(w2), 0, "e4m3").T @ x_hz
    xq = unpack_weight(x_words, x_scales)[:, unstriped(offs)]
    y = mxq(f64(w1), 0, "e4m3").T @ xq
    ra = d[:, unstriped(n2)] - (0.5 * y[:, unstriped(n1)])
    ds = y.copy()
    ds[:, unstriped(n1)] = ra
    z = f64(gn) * ds
    h = mxq(f64(w3), 0, "e4m3").T @ mxq(z, 0, "e4m3")
    sm = np.maximum(h, h[np.arange(N)[:, None], runs(n4, N)])
    ds2 = np.zeros((N, S))
    ds2[np.arange(N)[:, None], runs(n3, N)] = sm
    return ds2 * sigmoid(h)

@@ -1,0 +1,180 @@
+import concourse.mybir as mybir
+
+K, T, S, N, H, W = 512, 2048, 512, 512, 512, 256
+FLOPS = 3 * 2 * 512 * 512 * 512
+
+F32 = mybir.dt.float32
+BF16 = mybir.dt.bfloat16
+I32 = mybir.dt.int32
+U32 = mybir.dt.uint32
+U16 = mybir.dt.uint16
+U8 = mybir.dt.uint8
+FP8X4 = mybir.dt.float8_e4m3fn_x4
+COPY = mybir.ActivationFunctionType.Copy
+SIGMOID = mybir.ActivationFunctionType.Sigmoid
+ADD = mybir.AluOpType.add
+MULT = mybir.AluOpType.mult
+MAX = mybir.AluOpType.max
+SUB = mybir.AluOpType.subtract
+
+P = 128
+PACK = 4
+
+
+def tile_picked_twhputbsendg_none_p_kernel(tc, x_words, x_scales, w1, w2, gn, w3, offs, hz, n1, n2, n3, n4, out):
+    nc = tc.nc
+    with (
+        tc.tile_pool(name="held", bufs=1) as held,
+        tc.psum_pool(name="psum", bufs=1) as psum,
+    ):
+        def load_list(src, name):
+            tile = held.tile([P, src.shape[1]], U16, name=name)
+            nc.sync.dma_start(tile[:], src)
+            return tile
+
+        def load_weight(w, name, tag):
+            raw = held.tile([P, PACK, 512], F32, name=name, tag=tag)
+            nc.sync.dma_start(raw[:], w.rearrange("(p j) c -> p j c", j=PACK))
+            return raw
+
+        def deal(copy, raw, u, name, tag):
+            grouped = held.tile([P, 2, P, PACK], BF16, name=name, tag=tag, align_bytes=64)
+            src = raw[:].rearrange("p j (m t) -> p m j t", t=PACK)[:, :, :, 2 * u : 2 * u + 2]
+            copy(grouped[:].rearrange("p t m j -> p m j t"), src)
+            return grouped
+
+        def quantize_half(grouped, name):
+            codes = held.tile([P, 2 * P], U32, name=name + "_codes", align_bytes=64)
+            scales = held.tile([P, 2 * P], U8, name=name + "_scales", align_bytes=64)
+            nc.vector.quantize_mx(out=codes[:].bitcast(FP8X4), scales=scales[:], in_=grouped[:].rearrange("p t m j -> p (t m j)"))
+            return codes, scales
+
+        def product(halves, t, rhs_codes, rhs_scales, bank):
+            codes, scales = halves[t // 2]
+            cols = slice((t % 2) * P, (t % 2 + 1) * P)
+            acc = psum.tile([P, rhs_scales.shape[1]], F32, name="bank%d" % bank)
+            nc.tensor.matmul_mx(out=acc[:], lhsT=codes[:, cols].bitcast(FP8X4), lhsT_scale=scales[:, cols],
+                                rhs=rhs_codes.bitcast(FP8X4), rhs_scale=rhs_scales, start=True, stop=True)
+            return acc
+
+        xs = held.tile([P, T], U8, name="xs", tag="raw_b")
+        xs_words = xs[:].bitcast(I32)
+        nc.vector.memset(xs_words[:, 0:256], 0)
+        nc.gpsimd.memset(xs_words[:, 256:512], 0)
+        offs_sb = load_list(offs, "offs_sb")
+        hz_sb = load_list(hz, "hz_sb")
+        xs_rows = x_scales[0].bitcast(I32)
+        for e in range(2):
+            nc.sync.dma_start(xs_words[e:P:16, :], xs_rows[e:16:2, :])
+        gain = held.tile([P, PACK], F32, name="gain")
+        nc.sync.dma_start(gain[:], gn.rearrange("(p t) o -> p (t o)", t=PACK))
+        n1_sb = load_list(n1, "n1_sb")
+        xw = held.tile([P, T], U32, name="xw")
+        nc.sync.dma_start(xw[:].bitcast(I32), x_words[0].rearrange("p c r -> p (c r)").bitcast(I32))
+        w1_raw = load_weight(w1, "w1_raw", "raw_a")
+        n2_sb = load_list(n2, "n2_sb")
+        n4_sb = load_list(n4, "n4_sb")
+        n3_sb = load_list(n3, "n3_sb")
+
+        gain2 = held.tile([P, PACK], F32, name="gain2")
+        nc.scalar.activation(gain2[:], gain[:], COPY, scale=2.0)
+
+        planes = []
+        for name, lists in (("offs", offs_sb), ("hz", hz_sb)):
+            picked = held.tile([P, S], U8, name="picked_" + name)
+            nc.vector.tensor_copy(picked[:], xs[:].indirect(lists[:]))
+            plane = held.tile([P, S], U8, name="plane_" + name, align_bytes=64)
+            nc.vector.tensor_copy(plane[:].bitcast(I32), picked[:].bitcast(I32))
+            for e in range(2):
+                nc.scalar.dma_start(plane[:].bitcast(I32)[2 + e : P : 32, :], picked[:].bitcast(I32)[16 + e : P : 32, :])
+            planes.append(plane)
+        w2_raw = load_weight(w2, "w2_raw", "raw_b")
+        xq = held.tile([P, S], U32, name="xq", align_bytes=64)
+        nc.vector.tensor_copy(xq[:], xw[:].indirect(offs_sb[:]))
+        xh = held.tile([P, S], U32, name="xh", align_bytes=64)
+        nc.vector.tensor_copy(xh[:], xw[:].indirect(hz_sb[:]))
+
+        w1_g = [deal(nc.scalar.copy, w1_raw, u, "w1_g%d" % u, "w1_g%d" % u) for u in range(2)]
+        w1_q = [quantize_half(w1_g[u], "w1_q%d" % u) for u in range(2)]
+        w3_raw = load_weight(w3, "w3_raw", "raw_a")
+
+        z = []
+        for t in range(PACK):
+            y_acc = product(w1_q, t, xq[:], planes[0][:], t)
+            z_t = held.tile([P, S], F32, name="z%d" % t)
+            nc.scalar.activation(z_t[:], y_acc[:], COPY, scale=gain[:, t : t + 1])
+            z.append(z_t)
+
+        w2_g = [deal(nc.vector.tensor_copy, w2_raw, u, "w2_g%d" % u, "w2_g%d" % u) for u in range(2)]
+        w2_q = [quantize_half(w2_g[u], "w2_q%d" % u) for u in range(2)]
+
+        own = held.tile([P, PACK, W], F32, name="own", tag="w2_g1", align_bytes=64)
+        d_acc = [product(w2_q, t, xh[:], planes[1][:], PACK + t) for t in range(PACK)]
+        d = [held.tile([P, S], F32, name="d%d" % t, tag="d%d" % t, align_bytes=64) for t in range(PACK)]
+        for t in range(PACK - 1):
+            nc.scalar.activation(d[t][:], d_acc[t][:], COPY, scale=gain2[:, t : t + 1])
+        for t in range(PACK):
+            nc.vector.tensor_copy(own[:, t, :], z[t][:].indirect(n1_sb[:]))
+            if t == PACK - 1:
+                nc.vector.tensor_scalar(d[t][:], d_acc[t][:], gain2[:, t : t + 1], None, MULT)
+            ra2 = held.tile([P, W], F32, name="ra2_%d" % t)
+            nc.vector.tensor_tensor(ra2[:], d[t][:].indirect(n2_sb[:]), own[:, t, :], SUB)
+            nc.scalar.activation(z[t][:].indirect(n1_sb[:]), ra2[:], COPY, scale=0.5)
+
+        w3_g = [deal(nc.vector.tensor_copy, w3_raw, u, "w3_g%d" % u, "d%d" % (2 + u)) for u in range(2)]
+        w3_q = [quantize_half(w3_g[u], "w3_q%d" % u) for u in range(2)]
+
+        pairs = held.tile([P, 2, S, 2], BF16, name="pairs", tag="w2_g1", align_bytes=64)
+        for t in range(PACK):
+            nc.vector.tensor_copy(pairs[:, t // 2, :, t % 2], z[t][:])
+        pair_words = pairs[:].rearrange("p u j e -> p u (j e)").bitcast(I32)
+        halves = [slice(0, S // 2), slice(S // 2, S)]
+        z_codes = held.tile([P, S], U32, name="z_codes", align_bytes=64)
+        z_scales = held.tile([P, S], U8, name="z_scales", align_bytes=64)
+        woven = []
+        for c in range(2):
+            wv = held.tile([P, (S // 2) * PACK], BF16, name="woven%d" % c, align_bytes=64)
+            nc.vector.tensor_copy(wv[:].bitcast(I32).rearrange("p (j u) -> p j u", u=2), pair_words[:, :, halves[c]].rearrange("p u j -> p j u"))
+            woven.append(wv)
+        for c in range(2):
+            nc.vector.quantize_mx(out=z_codes[:, halves[c]].bitcast(FP8X4), scales=z_scales[:, halves[c]], in_=woven[c][:])
+
+        out_rows = out.rearrange("(p t) j -> p t j", t=PACK)
+        h, ds2 = [], []
+
+        def finish(t):
+            gate = held.tile([P, S], F32, name="gate%d" % t)
+            nc.scalar.activation(gate[:], h[t][:], SIGMOID)
+            res = held.tile([P, S], F32, name="res%d" % t)
+            nc.vector.tensor_tensor(res[:], ds2[t][:, 0:S], gate[:], MULT)
+            nc.sync.dma_start(out_rows[:, t, :], res[:])
+
+        for t in range(PACK):
+            h_t = held.tile([P, S], F32, name="h%d" % t)
+            h.append(h_t)
+            if t == 0:
+                accs = [product(w3_q, t, z_codes[:, halves[c]], z_scales[:, halves[c]], c) for c in range(2)]
+                for c in range(2):
+                    nc.scalar.copy(h_t[:, halves[c]], accs[c][:])
+                window = held.tile([P, S], F32, name="ds2_%d" % t)
+                others = [held.tile([P, S // 2], F32, name="other0_%d" % c) for c in range(2)]
+                nc.vector.tensor_copy(others[0][:], h_t[:].indirect(n4_sb[:, 0:16]))
+                nc.scalar.activation(others[1][:], h_t[:].indirect(n4_sb[:, 16:32]), COPY)
+                for c in range(2):
+                    sm = held.tile([P, S // 2], F32, name="sm0_%d" % c)
+                    nc.vector.tensor_tensor(sm[:], accs[c][:], others[c][:], MAX)
+                    nc.vector.tensor_copy(window[:].indirect(n3_sb[:, 16 * c : 16 * c + 16]), sm[:])
+            else:
+                h_acc = product(w3_q, t, z_codes[:], z_scales[:], 1 + t)
+                nc.scalar.copy(h_t[:], h_acc[:])
+                other = held.tile([P, S], F32, name="other%d" % t)
+                for c in range(2):
+                    nc.scalar.activation(other[:, halves[c]], h_t[:].indirect(n4_sb[:, 16 * c : 16 * c + 16]), COPY)
+                sm = held.tile([P, S], F32, name="sm%d" % t)
+                nc.vector.tensor_tensor(sm[:], h_acc[:], other[:], MAX)
+                window = held.tile([P, 2 * S], F32, name="ds2_%d" % t)
+                nc.vector.tensor_copy(window[:].indirect(n3_sb[:]), sm[:])
+            ds2.append(window)
+            if t > 0:
+                finish(t - 1)
+        finish(PACK - 1)

@@ -69,9 +69,9 @@ def tile_picked_twhputbsendg_none_p_kernel(tc, x_words, x_scales, w1, w2, gn, w3
         gain = held.tile([P, PACK], F32, name="gain")
         nc.sync.dma_start(gain[:], gn.rearrange("(p t) o -> p (t o)", t=PACK))
         n1_sb = load_list(n1, "n1_sb")
+        w1_raw = load_weight(w1, "w1_raw", "raw_a")
         xw = held.tile([P, T], U32, name="xw")
         nc.sync.dma_start(xw[:].bitcast(I32), x_words[0].rearrange("p c r -> p (c r)").bitcast(I32))
-        w1_raw = load_weight(w1, "w1_raw", "raw_a")
         n2_sb = load_list(n2, "n2_sb")
         n4_sb = load_list(n4, "n4_sb")
         n3_sb = load_list(n3, "n3_sb")
@@ -86,17 +86,17 @@ def tile_picked_twhputbsendg_none_p_kernel(tc, x_words, x_scales, w1, w2, gn, w3
             plane = held.tile([P, S], U8, name="plane_" + name, align_bytes=64)
             nc.vector.tensor_copy(plane[:].bitcast(I32), picked[:].bitcast(I32))
             for e in range(2):
-                nc.scalar.dma_start(plane[:].bitcast(I32)[2 + e : P : 32, :], picked[:].bitcast(I32)[16 + e : P : 32, :])
+                nc.sync.dma_start(plane[:].bitcast(I32)[2 + e : P : 32, :], picked[:].bitcast(I32)[16 + e : P : 32, :])
             planes.append(plane)
         w2_raw = load_weight(w2, "w2_raw", "raw_b")
-        xq = held.tile([P, S], U32, name="xq", align_bytes=64)
-        nc.vector.tensor_copy(xq[:], xw[:].indirect(offs_sb[:]))
-        xh = held.tile([P, S], U32, name="xh", align_bytes=64)
-        nc.vector.tensor_copy(xh[:], xw[:].indirect(hz_sb[:]))
-
         w1_g = [deal(nc.scalar.copy, w1_raw, u, "w1_g%d" % u, "w1_g%d" % u) for u in range(2)]
         w1_q = [quantize_half(w1_g[u], "w1_q%d" % u) for u in range(2)]
         w3_raw = load_weight(w3, "w3_raw", "raw_a")
+
+        xq = held.tile([P, S], U32, name="xq", tag="w1_g0", align_bytes=64)
+        nc.vector.tensor_copy(xq[:], xw[:].indirect(offs_sb[:]))
+        xh = held.tile([P, S], U32, name="xh", tag="w1_g1", align_bytes=64)
+        nc.vector.tensor_copy(xh[:], xw[:].indirect(hz_sb[:]))
 
         z = []
         for t in range(PACK):
@@ -108,33 +108,36 @@ def tile_picked_twhputbsendg_none_p_kernel(tc, x_words, x_scales, w1, w2, gn, w3
         w2_g = [deal(nc.vector.tensor_copy, w2_raw, u, "w2_g%d" % u, "w2_g%d" % u) for u in range(2)]
         w2_q = [quantize_half(w2_g[u], "w2_q%d" % u) for u in range(2)]
 
-        own = held.tile([P, PACK, W], F32, name="own", tag="w2_g1", align_bytes=64)
         d_acc = [product(w2_q, t, xh[:], planes[1][:], PACK + t) for t in range(PACK)]
         d = [held.tile([P, S], F32, name="d%d" % t, tag="d%d" % t, align_bytes=64) for t in range(PACK)]
         for t in range(PACK - 1):
             nc.scalar.activation(d[t][:], d_acc[t][:], COPY, scale=gain2[:, t : t + 1])
         for t in range(PACK):
-            nc.vector.tensor_copy(own[:, t, :], z[t][:].indirect(n1_sb[:]))
+            own = held.tile([P, W], F32, name="own%d" % t, tag="w2_g%d" % (t % 2), align_bytes=64)
+            nc.vector.tensor_copy(own[:], z[t][:].indirect(n1_sb[:]))
             if t == PACK - 1:
                 nc.vector.tensor_scalar(d[t][:], d_acc[t][:], gain2[:, t : t + 1], None, MULT)
             ra2 = held.tile([P, W], F32, name="ra2_%d" % t)
-            nc.vector.tensor_tensor(ra2[:], d[t][:].indirect(n2_sb[:]), own[:, t, :], SUB)
+            nc.vector.tensor_tensor(ra2[:], d[t][:].indirect(n2_sb[:]), own[:], SUB)
             nc.scalar.activation(z[t][:].indirect(n1_sb[:]), ra2[:], COPY, scale=0.5)
 
-        w3_g = [deal(nc.vector.tensor_copy, w3_raw, u, "w3_g%d" % u, "d%d" % (2 + u)) for u in range(2)]
-        w3_q = [quantize_half(w3_g[u], "w3_q%d" % u) for u in range(2)]
+        w3_q = [quantize_half(deal(nc.vector.tensor_copy, w3_raw, 0, "w3_g0", "d3"), "w3_q0")]
 
         pairs = held.tile([P, 2, S, 2], BF16, name="pairs", tag="w2_g1", align_bytes=64)
         for t in range(PACK):
             nc.vector.tensor_copy(pairs[:, t // 2, :, t % 2], z[t][:])
-        pair_words = pairs[:].rearrange("p u j e -> p u (j e)").bitcast(I32)
+        pair_words = pairs[:].rearrange("p u j e -> p u (j e)").bitcast(U32)
         halves = [slice(0, S // 2), slice(S // 2, S)]
         z_codes = held.tile([P, S], U32, name="z_codes", align_bytes=64)
         z_scales = held.tile([P, S], U8, name="z_scales", align_bytes=64)
         woven = []
         for c in range(2):
-            wv = held.tile([P, (S // 2) * PACK], BF16, name="woven%d" % c, align_bytes=64)
-            nc.vector.tensor_copy(wv[:].bitcast(I32).rearrange("p (j u) -> p j u", u=2), pair_words[:, :, halves[c]].rearrange("p u j -> p j u"))
+            wv = held.tile([P, (S // 2) * PACK], BF16, name="woven%d" % c, tag="woven%d" % c, align_bytes=64)
+            src = pair_words[:, :, halves[c]].rearrange("p u j -> p j u")
+            if c == 0:
+                nc.vector.tensor_copy(wv[:].bitcast(I32).rearrange("p (j u) -> p j u", u=2), pairs[:].rearrange("p u j e -> p u (j e)").bitcast(I32)[:, :, halves[c]].rearrange("p u j -> p j u"))
+            else:
+                nc.scalar.copy(wv[:].bitcast(U32).rearrange("p (j u) -> p j u", u=2), src)
             woven.append(wv)
         for c in range(2):
             nc.vector.quantize_mx(out=z_codes[:, halves[c]].bitcast(FP8X4), scales=z_scales[:, halves[c]], in_=woven[c][:])
@@ -145,9 +148,15 @@ def tile_picked_twhputbsendg_none_p_kernel(tc, x_words, x_scales, w1, w2, gn, w3
         def finish(t):
             gate = held.tile([P, S], F32, name="gate%d" % t)
             nc.scalar.activation(gate[:], h[t][:], SIGMOID)
-            res = held.tile([P, S], F32, name="res%d" % t)
-            nc.vector.tensor_tensor(res[:], ds2[t][:, 0:S], gate[:], MULT)
-            nc.sync.dma_start(out_rows[:, t, :], res[:])
+            if t < PACK - 1:
+                res = held.tile([P, S], F32, name="res%d" % t)
+                nc.gpsimd.tensor_tensor(res[:], ds2[t][:, 0:S], gate[:], MULT)
+                nc.sync.dma_start(out_rows[:, t, :], res[:])
+            else:
+                for c in range(2):
+                    res = held.tile([P, S // 2], F32, name="res%d_%d" % (t, c))
+                    nc.vector.tensor_tensor(res[:], ds2[t][:, halves[c]], gate[:, halves[c]], MULT)
+                    nc.sync.dma_start(out_rows[:, t, halves[c]], res[:])
 
         for t in range(PACK):
             h_t = held.tile([P, S], F32, name="h%d" % t)
@@ -156,6 +165,7 @@ def tile_picked_twhputbsendg_none_p_kernel(tc, x_words, x_scales, w1, w2, gn, w3
                 accs = [product(w3_q, t, z_codes[:, halves[c]], z_scales[:, halves[c]], c) for c in range(2)]
                 for c in range(2):
                     nc.scalar.copy(h_t[:, halves[c]], accs[c][:])
+                w3_q.append(quantize_half(deal(nc.vector.tensor_copy, w3_raw, 1, "w3_g1", "woven1"), "w3_q1"))
                 window = held.tile([P, S], F32, name="ds2_%d" % t)
                 others = [held.tile([P, S // 2], F32, name="other0_%d" % c) for c in range(2)]
                 nc.vector.tensor_copy(others[0][:], h_t[:].indirect(n4_sb[:, 0:16]))

@@ -11,6 +11,7 @@ U16 = mybir.dt.uint16
 U8 = mybir.dt.uint8
 FP8X4 = mybir.dt.float8_e4m3fn_x4
 COPY = mybir.ActivationFunctionType.Copy
+RELU = mybir.ActivationFunctionType.Relu
 SIGMOID = mybir.ActivationFunctionType.Sigmoid
 ADD = mybir.AluOpType.add
 MULT = mybir.AluOpType.mult
@@ -79,17 +80,15 @@ def tile_picked_twhputbsendg_none_p_kernel(tc, x_words, x_scales, w1, w2, gn, w3
         gain2 = held.tile([P, PACK], F32, name="gain2")
         nc.scalar.activation(gain2[:], gain[:], COPY, scale=2.0)
 
-        planes = []
-        for name, lists in (("offs", offs_sb), ("hz", hz_sb)):
-            picked = held.tile([P, S], U8, name="picked_" + name)
-            nc.vector.tensor_copy(picked[:], xs[:].indirect(lists[:]))
-            plane = held.tile([P, S], U8, name="plane_" + name, align_bytes=64)
-            nc.vector.tensor_copy(plane[:].bitcast(I32), picked[:].bitcast(I32))
-            for e in range(2):
-                nc.sync.dma_start(plane[:].bitcast(I32)[2 + e : P : 32, :], picked[:].bitcast(I32)[16 + e : P : 32, :])
-            planes.append(plane)
+        picked = held.tile([P, 2 * S], U8, name="picked")
+        nc.vector.tensor_copy(picked[:, 0:S], xs[:].indirect(offs_sb[:]))
+        nc.vector.tensor_copy(picked[:, S : 2 * S], xs[:].indirect(hz_sb[:]))
+        x_plane = held.tile([P, 2 * S], U8, name="x_plane", align_bytes=64)
+        nc.vector.tensor_copy(x_plane[:].bitcast(I32), picked[:].bitcast(I32))
+        for e in range(2):
+            nc.sync.dma_start(x_plane[:].bitcast(I32)[2 + e : P : 32, :], picked[:].bitcast(I32)[16 + e : P : 32, :])
         w2_raw = load_weight(w2, "w2_raw", "raw_b")
-        w1_g = [deal(nc.scalar.copy, w1_raw, u, "w1_g%d" % u, "w1_g%d" % u) for u in range(2)]
+        w1_g = [deal(copy, w1_raw, u, "w1_g%d" % u, "w1_g%d" % u) for u, copy in enumerate((nc.vector.tensor_copy, nc.scalar.copy))]
         w1_q = [quantize_half(w1_g[u], "w1_q%d" % u) for u in range(2)]
         w3_raw = load_weight(w3, "w3_raw", "raw_a")
 
@@ -100,7 +99,7 @@ def tile_picked_twhputbsendg_none_p_kernel(tc, x_words, x_scales, w1, w2, gn, w3
 
         z = []
         for t in range(PACK):
-            y_acc = product(w1_q, t, xq[:], planes[0][:], t)
+            y_acc = product(w1_q, t, xq[:], x_plane[:, 0:S], t)
             z_t = held.tile([P, S], F32, name="z%d" % t)
             nc.scalar.activation(z_t[:], y_acc[:], COPY, scale=gain[:, t : t + 1])
             z.append(z_t)
@@ -108,7 +107,7 @@ def tile_picked_twhputbsendg_none_p_kernel(tc, x_words, x_scales, w1, w2, gn, w3
         w2_g = [deal(nc.vector.tensor_copy, w2_raw, u, "w2_g%d" % u, "w2_g%d" % u) for u in range(2)]
         w2_q = [quantize_half(w2_g[u], "w2_q%d" % u) for u in range(2)]
 
-        d_acc = [product(w2_q, t, xh[:], planes[1][:], PACK + t) for t in range(PACK)]
+        d_acc = [product(w2_q, t, xh[:], x_plane[:, S : 2 * S], PACK + t) for t in range(PACK)]
         d = [held.tile([P, S], F32, name="d%d" % t, tag="d%d" % t, align_bytes=64) for t in range(PACK)]
         for t in range(PACK - 1):
             nc.scalar.activation(d[t][:], d_acc[t][:], COPY, scale=gain2[:, t : t + 1])
@@ -149,7 +148,7 @@ def tile_picked_twhputbsendg_none_p_kernel(tc, x_words, x_scales, w1, w2, gn, w3
             gate = held.tile([P, S], F32, name="gate%d" % t)
             nc.scalar.activation(gate[:], h[t][:], SIGMOID)
             if t < PACK - 1:
-                res = held.tile([P, S], F32, name="res%d" % t)
+                res = held.tile([P, S], F32, name="res%d" % t, tag=("res0", "other3", "excess")[t])
                 nc.gpsimd.tensor_tensor(res[:], ds2[t][:, 0:S], gate[:], MULT)
                 nc.sync.dma_start(out_rows[:, t, :], res[:])
             else:
@@ -177,14 +176,22 @@ def tile_picked_twhputbsendg_none_p_kernel(tc, x_words, x_scales, w1, w2, gn, w3
             else:
                 h_acc = product(w3_q, t, z_codes[:], z_scales[:], 1 + t)
                 nc.scalar.copy(h_t[:], h_acc[:])
-                other = held.tile([P, S], F32, name="other%d" % t)
+                other = held.tile([P, S], F32, name="other%d" % t, tag="other%d" % t)
                 for c in range(2):
                     nc.scalar.activation(other[:, halves[c]], h_t[:].indirect(n4_sb[:, 16 * c : 16 * c + 16]), COPY)
                 sm = held.tile([P, S], F32, name="sm%d" % t)
-                nc.vector.tensor_tensor(sm[:], h_acc[:], other[:], MAX)
+                if t < PACK - 1:
+                    nc.vector.tensor_tensor(sm[:], h_acc[:], other[:], MAX)
+                else:
+                    diff = held.tile([P, S], F32, name="diff")
+                    nc.gpsimd.tensor_tensor(diff[:], other[:], h_t[:], SUB)
+                    excess = held.tile([P, S], F32, name="excess", tag="excess")
+                    nc.scalar.activation(excess[:], diff[:], RELU)
+                    nc.gpsimd.tensor_tensor(sm[:], h_t[:], excess[:], ADD)
                 window = held.tile([P, 2 * S], F32, name="ds2_%d" % t)
                 nc.vector.tensor_copy(window[:].indirect(n3_sb[:]), sm[:])
             ds2.append(window)
-            if t > 0:
-                finish(t - 1)
-        finish(PACK - 1)
+            if t == 2:
+                finish(0)
+        for t in range(1, PACK):
+            finish(t)

@@ -77,6 +77,8 @@ def tile_picked_twhputbsendg_none_p_kernel(tc, x_words, x_scales, w1, w2, gn, w3
         n4_sb = load_list(n4, "n4_sb")
         n3_sb = load_list(n3, "n3_sb")
 
+        warm = held.tile([P, 1], F32, name="warm")
+        nc.scalar.activation(warm[:], gain[:, 0:1], SIGMOID)
         gain2 = held.tile([P, PACK], F32, name="gain2")
         nc.scalar.activation(gain2[:], gain[:], COPY, scale=2.0)
 
@@ -109,21 +111,27 @@ def tile_picked_twhputbsendg_none_p_kernel(tc, x_words, x_scales, w1, w2, gn, w3
 
         d_acc = [product(w2_q, t, xh[:], x_plane[:, S : 2 * S], PACK + t) for t in range(PACK)]
         d = [held.tile([P, S], F32, name="d%d" % t, tag="d%d" % t, align_bytes=64) for t in range(PACK)]
-        for t in range(PACK - 1):
-            nc.scalar.activation(d[t][:], d_acc[t][:], COPY, scale=gain2[:, t : t + 1])
+        last = PACK - 1
+        less_half = held.tile([P, W], F32, name="less_half")
+        nc.scalar.activation(less_half[:], z[last][:].indirect(n1_sb[:]), COPY, scale=-0.5)
         for t in range(PACK):
-            own = held.tile([P, W], F32, name="own%d" % t, tag="w2_g%d" % (t % 2), align_bytes=64)
-            nc.vector.tensor_copy(own[:], z[t][:].indirect(n1_sb[:]))
-            if t == PACK - 1:
-                nc.vector.tensor_scalar(d[t][:], d_acc[t][:], gain2[:, t : t + 1], None, MULT)
+            nc.scalar.activation(d[t][:], d_acc[t][:], COPY, scale=(gain2 if t < last else gain)[:, t : t + 1])
+        own_a = held.tile([P, W], F32, name="own_a", tag="w2_g0", align_bytes=64)
+        own_b = held.tile([P, 2, W], F32, name="own_b", tag="w2_g1", align_bytes=64)
+        own = [own_a[:], own_b[:, 0, :], own_b[:, 1, :]]
+        for t in range(last):
+            nc.vector.tensor_copy(own[t], z[t][:].indirect(n1_sb[:]))
+        for t in range(last):
             ra2 = held.tile([P, W], F32, name="ra2_%d" % t)
-            nc.vector.tensor_tensor(ra2[:], d[t][:].indirect(n2_sb[:]), own[:], SUB)
+            nc.vector.tensor_tensor(ra2[:], d[t][:].indirect(n2_sb[:]), own[t], SUB)
             nc.scalar.activation(z[t][:].indirect(n1_sb[:]), ra2[:], COPY, scale=0.5)
+        w3_q = [quantize_half(deal(nc.vector.tensor_copy, w3_raw, 0, "w3_g0", "d2"), "w3_q0")]
+        fetched = held.tile([P, W], F32, name="fetched", tag="fetched", align_bytes=64)
+        nc.vector.tensor_copy(fetched[:], d[last][:].indirect(n2_sb[:]))
+        nc.vector.tensor_tensor(z[last][:].indirect(n1_sb[:]), fetched[:], less_half[:], ADD)
 
-        w3_q = [quantize_half(deal(nc.vector.tensor_copy, w3_raw, 0, "w3_g0", "d3"), "w3_q0")]
-
-        pairs = held.tile([P, 2, S, 2], BF16, name="pairs", tag="w2_g1", align_bytes=64)
-        for t in range(PACK):
+        pairs = held.tile([P, 2, S, 2], BF16, name="pairs", tag="fetched", align_bytes=64)
+        for t in (0, 1, 3, 2):
             nc.vector.tensor_copy(pairs[:, t // 2, :, t % 2], z[t][:])
         pair_words = pairs[:].rearrange("p u j e -> p u (j e)").bitcast(U32)
         halves = [slice(0, S // 2), slice(S // 2, S)]

import concourse.mybir as mybir

K, T, S, N, H, W = 512, 2048, 512, 512, 512, 256
FLOPS = 3 * 2 * 512 * 512 * 512

F32 = mybir.dt.float32
BF16 = mybir.dt.bfloat16
I32 = mybir.dt.int32
U32 = mybir.dt.uint32
U16 = mybir.dt.uint16
U8 = mybir.dt.uint8
FP8X4 = mybir.dt.float8_e4m3fn_x4
COPY = mybir.ActivationFunctionType.Copy
RELU = mybir.ActivationFunctionType.Relu
SIGMOID = mybir.ActivationFunctionType.Sigmoid
ADD = mybir.AluOpType.add
MULT = mybir.AluOpType.mult
MAX = mybir.AluOpType.max
SUB = mybir.AluOpType.subtract

P = 128
PACK = 4


def tile_picked_twhputbsendg_none_p_kernel(tc, x_words, x_scales, w1, w2, gn, w3, offs, hz, n1, n2, n3, n4, out):
    nc = tc.nc
    with (
        tc.tile_pool(name="held", bufs=1) as held,
        tc.psum_pool(name="psum", bufs=1) as psum,
    ):
        def load_list(src, name):
            tile = held.tile([P, src.shape[1]], U16, name=name)
            nc.sync.dma_start(tile[:], src)
            return tile

        def load_weight(w, name, tag):
            raw = held.tile([P, PACK, 512], F32, name=name, tag=tag)
            nc.sync.dma_start(raw[:], w.rearrange("(p j) c -> p j c", j=PACK))
            return raw

        def deal(copy, raw, u, name, tag):
            grouped = held.tile([P, 2, P, PACK], BF16, name=name, tag=tag, align_bytes=64)
            src = raw[:].rearrange("p j (m t) -> p m j t", t=PACK)[:, :, :, 2 * u : 2 * u + 2]
            copy(grouped[:].rearrange("p t m j -> p m j t"), src)
            return grouped

        def quantize_half(grouped, name):
            codes = held.tile([P, 2 * P], U32, name=name + "_codes", align_bytes=64)
            scales = held.tile([P, 2 * P], U8, name=name + "_scales", align_bytes=64)
            nc.vector.quantize_mx(out=codes[:].bitcast(FP8X4), scales=scales[:], in_=grouped[:].rearrange("p t m j -> p (t m j)"))
            return codes, scales

        def product(halves, t, rhs_codes, rhs_scales, bank):
            codes, scales = halves[t // 2]
            cols = slice((t % 2) * P, (t % 2 + 1) * P)
            acc = psum.tile([P, rhs_scales.shape[1]], F32, name="bank%d" % bank)
            nc.tensor.matmul_mx(out=acc[:], lhsT=codes[:, cols].bitcast(FP8X4), lhsT_scale=scales[:, cols],
                                rhs=rhs_codes.bitcast(FP8X4), rhs_scale=rhs_scales, start=True, stop=True)
            return acc

        xs = held.tile([P, T], U8, name="xs", tag="raw_b")
        xs_words = xs[:].bitcast(I32)
        nc.vector.memset(xs_words[:, 0:256], 0)
        nc.gpsimd.memset(xs_words[:, 256:512], 0)
        offs_sb = load_list(offs, "offs_sb")
        hz_sb = load_list(hz, "hz_sb")
        xs_rows = x_scales[0].bitcast(I32)
        for e in range(2):
            nc.sync.dma_start(xs_words[e:P:16, :], xs_rows[e:16:2, :])
        gain = held.tile([P, PACK], F32, name="gain")
        nc.sync.dma_start(gain[:], gn.rearrange("(p t) o -> p (t o)", t=PACK))
        n1_sb = load_list(n1, "n1_sb")
        w1_raw = load_weight(w1, "w1_raw", "raw_a")
        xw = held.tile([P, T], U32, name="xw")
        nc.sync.dma_start(xw[:].bitcast(I32), x_words[0].rearrange("p c r -> p (c r)").bitcast(I32))
        n2_sb = load_list(n2, "n2_sb")
        n4_sb = load_list(n4, "n4_sb")
        n3_sb = load_list(n3, "n3_sb")

        warm = held.tile([P, 1], F32, name="warm")
        nc.scalar.activation(warm[:], gain[:, 0:1], SIGMOID)
        gain2 = held.tile([P, PACK], F32, name="gain2")
        nc.scalar.activation(gain2[:], gain[:], COPY, scale=2.0)

        picked = held.tile([P, 2 * S], U8, name="picked")
        nc.vector.tensor_copy(picked[:, 0:S], xs[:].indirect(offs_sb[:]))
        nc.vector.tensor_copy(picked[:, S : 2 * S], xs[:].indirect(hz_sb[:]))
        x_plane = held.tile([P, 2 * S], U8, name="x_plane", align_bytes=64)
        nc.vector.tensor_copy(x_plane[:].bitcast(I32), picked[:].bitcast(I32))
        for e in range(2):
            nc.sync.dma_start(x_plane[:].bitcast(I32)[2 + e : P : 32, :], picked[:].bitcast(I32)[16 + e : P : 32, :])
        w2_raw = load_weight(w2, "w2_raw", "raw_b")
        w1_g = [deal(copy, w1_raw, u, "w1_g%d" % u, "w1_g%d" % u) for u, copy in enumerate((nc.vector.tensor_copy, nc.scalar.copy))]
        w1_q = [quantize_half(w1_g[u], "w1_q%d" % u) for u in range(2)]
        w3_raw = load_weight(w3, "w3_raw", "raw_a")

        xq = held.tile([P, S], U32, name="xq", tag="w1_g0", align_bytes=64)
        nc.vector.tensor_copy(xq[:], xw[:].indirect(offs_sb[:]))
        xh = held.tile([P, S], U32, name="xh", tag="w1_g1", align_bytes=64)
        nc.vector.tensor_copy(xh[:], xw[:].indirect(hz_sb[:]))

        z = []
        for t in range(PACK):
            y_acc = product(w1_q, t, xq[:], x_plane[:, 0:S], t)
            z_t = held.tile([P, S], F32, name="z%d" % t)
            nc.scalar.activation(z_t[:], y_acc[:], COPY, scale=gain[:, t : t + 1])
            z.append(z_t)

        w2_g = [deal(nc.vector.tensor_copy, w2_raw, u, "w2_g%d" % u, "w2_g%d" % u) for u in range(2)]
        w2_q = [quantize_half(w2_g[u], "w2_q%d" % u) for u in range(2)]

        d_acc = [product(w2_q, t, xh[:], x_plane[:, S : 2 * S], PACK + t) for t in range(PACK)]
        d = [held.tile([P, S], F32, name="d%d" % t, tag="d%d" % t, align_bytes=64) for t in range(PACK)]
        last = PACK - 1
        less_half = held.tile([P, W], F32, name="less_half")
        nc.scalar.activation(less_half[:], z[last][:].indirect(n1_sb[:]), COPY, scale=-0.5)
        for t in range(PACK):
            nc.scalar.activation(d[t][:], d_acc[t][:], COPY, scale=(gain2 if t < last else gain)[:, t : t + 1])
        own_a = held.tile([P, W], F32, name="own_a", tag="w2_g0", align_bytes=64)
        own_b = held.tile([P, 2, W], F32, name="own_b", tag="w2_g1", align_bytes=64)
        own = [own_a[:], own_b[:, 0, :], own_b[:, 1, :]]
        for t in range(last):
            nc.vector.tensor_copy(own[t], z[t][:].indirect(n1_sb[:]))
        for t in range(last):
            ra2 = held.tile([P, W], F32, name="ra2_%d" % t)
            nc.vector.tensor_tensor(ra2[:], d[t][:].indirect(n2_sb[:]), own[t], SUB)
            nc.scalar.activation(z[t][:].indirect(n1_sb[:]), ra2[:], COPY, scale=0.5)
        w3_q = [quantize_half(deal(nc.vector.tensor_copy, w3_raw, 0, "w3_g0", "d2"), "w3_q0")]
        fetched = held.tile([P, W], F32, name="fetched", tag="fetched", align_bytes=64)
        nc.vector.tensor_copy(fetched[:], d[last][:].indirect(n2_sb[:]))
        nc.vector.tensor_tensor(z[last][:].indirect(n1_sb[:]), fetched[:], less_half[:], ADD)

        pairs = held.tile([P, 2, S, 2], BF16, name="pairs", tag="fetched", align_bytes=64)
        for t in (0, 1, 3, 2):
            nc.vector.tensor_copy(pairs[:, t // 2, :, t % 2], z[t][:])
        pair_words = pairs[:].rearrange("p u j e -> p u (j e)").bitcast(U32)
        halves = [slice(0, S // 2), slice(S // 2, S)]
        z_codes = held.tile([P, S], U32, name="z_codes", align_bytes=64)
        z_scales = held.tile([P, S], U8, name="z_scales", align_bytes=64)
        woven = []
        for c in range(2):
            wv = held.tile([P, (S // 2) * PACK], BF16, name="woven%d" % c, tag="woven%d" % c, align_bytes=64)
            src = pair_words[:, :, halves[c]].rearrange("p u j -> p j u")
            if c == 0:
                nc.vector.tensor_copy(wv[:].bitcast(I32).rearrange("p (j u) -> p j u", u=2), pairs[:].rearrange("p u j e -> p u (j e)").bitcast(I32)[:, :, halves[c]].rearrange("p u j -> p j u"))
            else:
                nc.scalar.copy(wv[:].bitcast(U32).rearrange("p (j u) -> p j u", u=2), src)
            woven.append(wv)
        for c in range(2):
            nc.vector.quantize_mx(out=z_codes[:, halves[c]].bitcast(FP8X4), scales=z_scales[:, halves[c]], in_=woven[c][:])

        out_rows = out.rearrange("(p t) j -> p t j", t=PACK)
        h, ds2 = [], []

        def finish(t):
            gate = held.tile([P, S], F32, name="gate%d" % t)
            nc.scalar.activation(gate[:], h[t][:], SIGMOID)
            if t < PACK - 1:
                res = held.tile([P, S], F32, name="res%d" % t, tag=("res0", "other3", "excess")[t])
                nc.gpsimd.tensor_tensor(res[:], ds2[t][:, 0:S], gate[:], MULT)
                nc.sync.dma_start(out_rows[:, t, :], res[:])
            else:
                for c in range(2):
                    res = held.tile([P, S // 2], F32, name="res%d_%d" % (t, c))
                    nc.vector.tensor_tensor(res[:], ds2[t][:, halves[c]], gate[:, halves[c]], MULT)
                    nc.sync.dma_start(out_rows[:, t, halves[c]], res[:])

        for t in range(PACK):
            h_t = held.tile([P, S], F32, name="h%d" % t)
            h.append(h_t)
            if t == 0:
                accs = [product(w3_q, t, z_codes[:, halves[c]], z_scales[:, halves[c]], c) for c in range(2)]
                for c in range(2):
                    nc.scalar.copy(h_t[:, halves[c]], accs[c][:])
                w3_q.append(quantize_half(deal(nc.vector.tensor_copy, w3_raw, 1, "w3_g1", "woven1"), "w3_q1"))
                window = held.tile([P, S], F32, name="ds2_%d" % t)
                others = [held.tile([P, S // 2], F32, name="other0_%d" % c) for c in range(2)]
                nc.vector.tensor_copy(others[0][:], h_t[:].indirect(n4_sb[:, 0:16]))
                nc.scalar.activation(others[1][:], h_t[:].indirect(n4_sb[:, 16:32]), COPY)
                for c in range(2):
                    sm = held.tile([P, S // 2], F32, name="sm0_%d" % c)
                    nc.vector.tensor_tensor(sm[:], accs[c][:], others[c][:], MAX)
                    nc.vector.tensor_copy(window[:].indirect(n3_sb[:, 16 * c : 16 * c + 16]), sm[:])
            else:
                h_acc = product(w3_q, t, z_codes[:], z_scales[:], 1 + t)
                nc.scalar.copy(h_t[:], h_acc[:])
                other = held.tile([P, S], F32, name="other%d" % t, tag="other%d" % t)
                for c in range(2):
                    nc.scalar.activation(other[:, halves[c]], h_t[:].indirect(n4_sb[:, 16 * c : 16 * c + 16]), COPY)
                sm = held.tile([P, S], F32, name="sm%d" % t)
                if t < PACK - 1:
                    nc.vector.tensor_tensor(sm[:], h_acc[:], other[:], MAX)
                else:
                    diff = held.tile([P, S], F32, name="diff")
                    nc.gpsimd.tensor_tensor(diff[:], other[:], h_t[:], SUB)
                    excess = held.tile([P, S], F32, name="excess", tag="excess")
                    nc.scalar.activation(excess[:], diff[:], RELU)
                    nc.gpsimd.tensor_tensor(sm[:], h_t[:], excess[:], ADD)
                window = held.tile([P, 2 * S], F32, name="ds2_%d" % t)
                nc.vector.tensor_copy(window[:].indirect(n3_sb[:]), sm[:])
            ds2.append(window)
            if t == 2:
                finish(0)
        for t in range(1, PACK):
            finish(t)
